import numpy as np
import ml_dtypes


def mxq(x, axis, fmt="e4m3"):
    dtype, down = {"e4m3": (ml_dtypes.float8_e4m3fn, 7), "e5m2": (ml_dtypes.float8_e5m2, 14)}[fmt]
    v = np.moveaxis(np.asarray(x, np.float32).astype(ml_dtypes.bfloat16).astype(np.float64), axis, -1)
    blocks = v.reshape(v.shape[:-1] + (-1, 32))
    amax = np.abs(blocks).max(-1, keepdims=True)
    byte = np.maximum(np.where(amax > 0, np.frexp(amax)[1] - 1 + 127, 0) - down, 1)
    scale = np.exp2(byte - 127.0)
    codes = (blocks / scale).astype(np.float32).astype(dtype).astype(np.float64)
    return np.moveaxis((codes * scale).reshape(v.shape), -1, axis)


WIDE = False


def mx_kscale(k):
    if not WIDE:
        return np.ones(k)
    levels = np.array([10, -10, 5, -5, 0])
    if k % 512:
        return np.exp2(np.random.permutation(np.resize(levels, k // 32))).repeat(32)
    a = np.empty((k // 512, 16))
    for p in range(k // 512):
        a[p, :8] = np.random.permutation(np.resize(levels, 8))
        for g in range(8):
            far = levels[np.abs(levels - a[p, g]) >= 10]
            a[p, g + 8] = far[np.random.randint(len(far))]
    return np.exp2(a.ravel()).repeat(32)


def f64(x):
    return np.asarray(x).astype(np.float64)


def striped(idx):
    return np.tile(idx.reshape(-1, 16).T, (8, 1)).astype(np.uint16)


def unstriped(offs):
    return offs[:16].T.reshape(-1).astype(np.int64)


E2M1 = np.array([0.0, 0.5, 1.0, 1.5, 2.0, 3.0, 4.0, 6.0, -0.0, -0.5, -1.0, -1.5, -2.0, -3.0, -4.0, -6.0])


def pack_weight(w, fmt):
    k, n = w.shape
    w = f64(np.asarray(w, np.float32).astype(ml_dtypes.bfloat16)).reshape(k // 32, 32, n)
    amax = np.abs(w).max(1)
    if fmt == "e4m3":
        byte = np.frexp(amax)[1] - 1 + 127 - 7
    else:
        mant, ex = np.frexp(amax / 6.0)
        byte = np.where(mant > 0.5, ex, ex - 1) + 127
    byte = np.clip(np.where(amax > 0, byte, 1), 1, 254)
    scaled = (w * np.exp2(127.0 - byte)[:, None, :]).reshape(k, n).astype(np.float32)
    by_word = np.ascontiguousarray(scaled.reshape(k // 512, 128, 4, n).transpose(0, 1, 3, 2))
    if fmt == "e4m3":
        words = by_word.astype(ml_dtypes.float8_e4m3fn).view(np.uint8)
    else:
        c = by_word.astype(ml_dtypes.float4_e2m1fn).view(np.uint8) & 0xF
        words = (c[..., 0::2] | (c[..., 1::2] << 4)).reshape(k // 512, 128, 2 * n)
    return np.ascontiguousarray(words), np.ascontiguousarray(byte.astype(np.uint8).reshape(k // 512, 16, n))


def unpack_weight(words, scales, fmt):
    g, _, n = scales.shape
    words = np.ascontiguousarray(words).reshape(g, 128, n, -1)
    if fmt == "e4m3":
        vals = words.view(ml_dtypes.float8_e4m3fn).astype(np.float64)
    else:
        nib = np.empty((g, 128, n, 4), np.uint8)
        nib[..., 0::2] = words & 0xF
        nib[..., 1::2] = words >> 4
        vals = E2M1[nib]
    vals = vals * np.repeat(np.exp2(scales.astype(np.float64) - 127.0), 8, axis=1)[..., None]
    return vals.transpose(0, 1, 3, 2).reshape(g * 512, n)


def planes(y):
    n, m = y.shape
    v = y.astype(np.float32).astype(ml_dtypes.bfloat16).astype(np.float64).reshape(n // 32, 32, m)
    top = np.abs(v).max(1)
    byte = np.clip(np.where(top > 0, np.frexp(top)[1] - 1 + 127 - 7, 1), 1, 254)
    codes = (v * np.exp2(127.0 - byte)[:, None, :]).reshape(n, m).astype(np.float32).astype(ml_dtypes.float8_e4m3fn).view(np.uint8)
    words = codes.reshape(n // 512, 128, 4, m).transpose(0, 1, 3, 2)
    return np.ascontiguousarray(words), np.ascontiguousarray(byte.astype(np.uint8).reshape(n // 512, 16, m))


def gelu(v):
    return 0.5 * v * (1.0 + np.tanh(np.sqrt(2.0 / np.pi) * (v + 0.044715 * v**3)))


K, T, E, C, H, N = 1024, 512, 2, 256, 512, 512


def by_expert(wq, xq):
    return np.concatenate([wq[e].T @ xq[:, e * C:(e + 1) * C] for e in range(E)], axis=1)


def setup_inputs():
    n = np.random.standard_normal
    s = mx_kscale(K)
    u = mx_kscale(H)
    slot_token = np.random.permutation(T)[:E * C]
    x = pack_weight(n((K, T)) * s[:, None], "e4m3")
    w = [pack_weight(m, "e2m1") for m in n((E, K, N)) / np.sqrt(K) / s[None, :, None]]
    wb = [pack_weight(m, "e4m3") for m in n((E, H, N)) / np.sqrt(H) / u[None, :, None]]
    return {
        "x_words": x[0],
        "x_scales": x[1],
        "w_words": np.stack([m[0] for m in w]),
        "w_scales": np.stack([m[1] for m in w]),
        "wa": (n((E, K, H)) / np.sqrt(K) / s[None, :, None] * u).astype(np.float32),
        "wb_words": np.stack([m[0] for m in wb]),
        "wb_scales": np.stack([m[1] for m in wb]),
        "gate": np.tile(np.random.uniform(0.2, 1.0, E * C), (128, 1)).astype(np.float32),
        "offs": striped(slot_token),
    }


def reference(x_words, x_scales, w_words, w_scales, wa, wb_words, wb_scales, gate, offs):
    w = np.stack([unpack_weight(w_words[e], w_scales[e], "e2m1") for e in range(E)])
    waq = mxq(f64(wa), 1, "e4m3")
    wb = np.stack([unpack_weight(wb_words[e], wb_scales[e], "e4m3") for e in range(E)])
    idx = unstriped(offs)
    xq = unpack_weight(x_words, x_scales, "e4m3")[:, idx]
    h = gelu(by_expert(waq, xq))
    y = by_expert(w, xq) + by_expert(wb, mxq(h, 0, "e4m3"))
    out = np.zeros((N, T))
    out[:, idx] = f64(gate[:1]) * y
    out_0 = out
    return (out_0,) + planes(out_0)

from contextlib import ExitStack

import concourse.mybir as mybir

K, T, E, C, H, N = 1024, 512, 2, 256, 512, 512
FLOPS = 2 * E * C * (K * H + K * N + H * N)

F32 = mybir.dt.float32
BF16 = mybir.dt.bfloat16
I32 = mybir.dt.int32
U32 = mybir.dt.uint32
U16 = mybir.dt.uint16
U8 = mybir.dt.uint8
FP8X4 = mybir.dt.float8_e4m3fn_x4
FP4X4 = mybir.dt.float4_e2m1fn_x4
MULT = mybir.AluOpType.mult
COPY = mybir.ActivationFunctionType.Copy
GELU = mybir.ActivationFunctionType.Gelu_apprx_tanh

P = 128
PACK = 4
PASSES = K // (P * PACK)
BLOCK = 128
BLOCKS = E * C // BLOCK
LIST_COL = 16


def tile_moe_elr_gelu_kernel(
    tc, x_words, x_scales, w_words, w_scales, wa, wb_words, wb_scales, gate, offs, out_0, out_1, out_2
):
    nc = tc.nc
    with ExitStack() as ctx:
        sb = ctx.enter_context(tc.tile_pool(name="sb", bufs=1))
        ps = ctx.enter_context(tc.psum_pool(name="ps", bufs=1))

        def tile(name, shape, dtype, tag=None):
            return sb.tile(shape, dtype, name=name, tag=tag or name, align_bytes=64)

        offsets = sb.tile([P, E * C // LIST_COL], U16, name="offsets")
        xw = tile("xw", [P, PASSES * T], U32)
        xs = tile("xs", [P, PASSES * T], U8)
        wa_raw = {}
        w_raw = {}
        ws_raw = tile("ws_raw", [P, E * PASSES * N], U8)
        wbs_raw = tile("wbs_raw", [P, N], U8)
        gate_sb = {}

        nc.vector.memset(xs[:].bitcast(I32), 0)
        nc.vector.memset(ws_raw[:].bitcast(I32), 0)
        nc.gpsimd.memset(wbs_raw[:].bitcast(I32), 0)

        def load_wa(e, s, tag=None):
            wa_raw[e, s] = tile(f"wa_raw{e}{s}", [P, PACK, H], F32, tag)
            rows = wa[e, s * P * PACK : (s + 1) * P * PACK, :]
            nc.sync.dma_start(wa_raw[e, s][:], rows.rearrange("(p j) c -> p j c", j=PACK))

        def load_w(e):
            w_raw[e] = tile(f"w_raw{e}", [P, PASSES, 2 * N], U8)
            nc.sync.dma_start(w_raw[e][:].bitcast(I32), w_words[e].rearrange("s p b -> p s b").bitcast(I32))

        def load_gate(e, tag=None):
            gate_sb[e] = tile(f"gate_sb{e}", [P, C], F32, tag)
            nc.sync.dma_start(gate_sb[e][:], gate[:, e * C : (e + 1) * C])

        nc.sync.dma_start(offsets[:], offs)
        nc.sync.dma_start(
            xw[:].bitcast(I32).rearrange("p (s t) -> p s t", s=PASSES),
            x_words.rearrange("s p t d -> p s (t d)").bitcast(I32),
        )
        load_w(0)
        for q in range(4):
            nc.sync.dma_start(
                xs[32 * q : 32 * q + 4, :].bitcast(I32).rearrange("r (s t) -> r s t", s=PASSES),
                x_scales.rearrange("s b t -> b s t")[4 * q : 4 * q + 4].bitcast(I32),
            )
        load_w(1)
        wb_raw = tile("wb_raw", [P, E, N], U32)
        nc.sync.dma_start(wb_raw[:].bitcast(I32), wb_words.rearrange("e s p n d -> p (e s) (n d)").bitcast(I32))
        for q in range(4):
            nc.sync.dma_start(
                ws_raw[32 * q : 32 * q + 4, :].bitcast(I32).rearrange("r (a n) -> r a n", a=E * PASSES),
                w_scales.rearrange("e s b n -> b (e s) n")[4 * q : 4 * q + 4].bitcast(I32),
            )
        load_wa(0, 0)
        load_wa(0, 1)
        load_gate(0)
        for q in range(4):
            nc.gpsimd.dma_start(
                wbs_raw[32 * q : 32 * q + 4 * E, :].bitcast(I32),
                wb_scales[:, 0, 4 * q : 4 * q + 4, :].bitcast(I32),
            )

        xg = [[tile(f"xg{e}{s}", [P, C], U32) for s in range(PASSES)] for e in range(E)]
        xgs = [[tile(f"xgs{e}{s}", [P, C], U8) for s in range(PASSES)] for e in range(E)]
        wa_bf = {}
        wa_c = [[tile(f"wa_c{e}{s}", [P, H], U32) for s in range(PASSES)] for e in range(E)]
        wa_s = [[tile(f"wa_s{e}{s}", [P, H], U8) for s in range(PASSES)] for e in range(E)]
        w_c = [tile(f"w_c{e}", [P, PASSES, 2 * N], U8) for e in range(E)]
        w_s = {}
        wb_c = [tile(f"wb_c{e}", [P, N], U32) for e in range(E)]
        wb_s = {}
        h_ps = [ps.tile([P, PACK, BLOCK], F32, name=f"h_ps{b}") for b in range(BLOCKS)]
        y_ps = [ps.tile([P, PACK, BLOCK], F32, name=f"y_ps{b}") for b in range(BLOCKS)]
        h_bf = [tile(f"h_bf{b}", [P, BLOCK, PACK], BF16) for b in range(BLOCKS)]
        h_c = [tile(f"h_c{b}", [P, BLOCK], U32) for b in range(BLOCKS)]
        h_s = [tile(f"h_s{b}", [P, BLOCK], U8) for b in range(BLOCKS)]
        y_sb = {}
        out_sb = [tile(f"out_sb{t}", [P, T], F32) for t in range(PACK)]

        def expert_list(e):
            return offsets[:, e * C // LIST_COL : (e + 1) * C // LIST_COL]

        def block_list(b):
            return offsets[:, b * BLOCK // LIST_COL : (b + 1) * BLOCK // LIST_COL]

        def gather_words(e):
            for s in range(PASSES):
                nc.vector.tensor_copy(xg[e][s][:], xw[:, s * T : (s + 1) * T].indirect(expert_list(e)))

        def gather_scales(e):
            for s in range(PASSES):
                nc.vector.tensor_copy(xgs[e][s][:], xs[:, s * T : (s + 1) * T].indirect(expert_list(e)))

        def round_wa(e, s, on_vector, tag=None):
            wa_bf[e, s] = tile(f"wa_bf{e}{s}", [P, PACK, P, PACK], BF16, tag)
            src = wa_raw[e, s][:].rearrange("p j (m t) -> p m j t", t=PACK)
            dst = wa_bf[e, s][:].rearrange("p t m j -> p m j t")
            if on_vector > 0:
                nc.vector.tensor_copy(dst[:, :on_vector], src[:, :on_vector])
            if on_vector < P:
                nc.scalar.copy(dst[:, on_vector:], src[:, on_vector:])

        def quantize_wa(e, s):
            nc.vector.quantize_mx(
                out=wa_c[e][s][:].bitcast(FP8X4),
                scales=wa_s[e][s][:],
                in_=wa_bf[e, s][:].rearrange("p t m j -> p (t m j)"),
            )

        def deal(copy, dst, src):
            copy(dst.rearrange("p s (t m) -> p s m t", t=PACK), src.rearrange("p s (m t) -> p s m t", t=PACK))

        def deal_w_words(e, copy):
            deal(copy, w_c[e][:].bitcast(U16), w_raw[e][:].bitcast(U16))

        def deal_wb_words(e, copy):
            copy(wb_c[e][:].rearrange("p (t m) -> p m t", t=PACK), wb_raw[:, e, :].rearrange("p (m t) -> p m t", t=PACK))

        def deal_w_scales(e, tag):
            w_s[e] = tile(f"w_s{e}", [P, PASSES, N], U8, tag)
            src = ws_raw[:, e * PASSES * N : (e + 1) * PASSES * N].rearrange("p (s n) -> p s n", s=PASSES)
            deal(nc.vector.tensor_copy, w_s[e][:], src)

        def deal_wb_scales(tag):
            wb_s[0] = tile("wb_s", [P, N], U8, tag)
            nc.vector.tensor_copy(
                wb_s[0][:].rearrange("p (t m) -> p m t", t=PACK), wbs_raw[:].rearrange("p (m t) -> p m t", t=PACK)
            )

        def slots(b):
            u = (b * BLOCK) % C
            return slice(u, u + BLOCK)

        def h_pass(b, s):
            e = b * BLOCK // C
            for t in range(PACK):
                cols = slice(t * P, (t + 1) * P)
                nc.tensor.matmul_mx(
                    out=h_ps[b][:, t, :],
                    lhsT=wa_c[e][s][:, cols].bitcast(FP8X4),
                    lhsT_scale=wa_s[e][s][:, cols],
                    rhs=xg[e][s][:, slots(b)].bitcast(FP8X4),
                    rhs_scale=xgs[e][s][:, slots(b)],
                    start=(s == 0 and t == 0),
                    stop=(s == PASSES - 1 and t == PACK - 1),
                )

        def frozen_passes(b):
            e = b * BLOCK // C
            for s in range(PASSES):
                for t in range(PACK):
                    nc.tensor.matmul_mx(
                        out=y_ps[b][:, t, :],
                        lhsT=w_c[e][:, s, 2 * t * P : 2 * (t + 1) * P].bitcast(FP4X4),
                        lhsT_scale=w_s[e][:, s, t * P : (t + 1) * P],
                        rhs=xg[e][s][:, slots(b)].bitcast(FP8X4),
                        rhs_scale=xgs[e][s][:, slots(b)],
                        start=(s == 0 and t == 0),
                        stop=False,
                    )

        def gelu(b):
            nc.scalar.activation(h_bf[b][:], h_ps[b][:].rearrange("p t j -> p j t"), GELU)

        def quantize_h(b):
            nc.vector.quantize_mx(
                out=h_c[b][:].bitcast(FP8X4), scales=h_s[b][:], in_=h_bf[b][:].rearrange("p j t -> p (j t)")
            )

        def adapter_pass(b):
            e = b * BLOCK // C
            for t in range(PACK):
                cols = slice(t * P, (t + 1) * P)
                nc.tensor.matmul_mx(
                    out=y_ps[b][:, t, :],
                    lhsT=wb_c[e][:, cols].bitcast(FP8X4),
                    lhsT_scale=wb_s[0][4 * e : P, cols],
                    rhs=h_c[b][:].bitcast(FP8X4),
                    rhs_scale=h_s[b][:],
                    start=False,
                    stop=(t == PACK - 1),
                )

        def gate_y(b, t0, t1, tag=None):
            y = tile(f"y_sb{b}{t0}", [P, t1 - t0, BLOCK], F32, tag)
            g = gate_sb[b * BLOCK // C][:, slots(b)].unsqueeze(1).to_broadcast([P, t1 - t0, BLOCK])
            nc.vector.tensor_tensor(y[:], y_ps[b][:, t0:t1, :], g, MULT)
            for t in range(t0, t1):
                y_sb[b, t] = y[:, t - t0, :]

        def scatter(b, t, on_vector):
            window = out_sb[t][:].indirect(block_list(b))
            if on_vector:
                nc.vector.tensor_copy(window, y_sb[b, t])
            else:
                nc.scalar.activation(window, y_sb[b, t], COPY)

        gather_words(0)
        gather_scales(0)
        gather_words(1)
        gather_scales(1)
        for e in range(E):
            deal_w_words(e, nc.scalar.copy)
        load_wa(1, 0, "w_raw1")
        for e in range(E):
            deal_wb_words(e, nc.scalar.copy)
        load_wa(1, 1, "wb_raw")
        round_wa(0, 0, 84)
        load_gate(1, "wa_raw00")
        quantize_wa(0, 0)
        h_pass(0, 0)
        h_pass(1, 0)
        round_wa(0, 1, 84)
        quantize_wa(0, 1)
        h_pass(0, 1)
        h_pass(1, 1)
        gelu(0)
        gelu(1)
        deal_w_scales(0, "wa_bf00")
        deal_wb_scales("wa_bf01")
        quantize_h(0)
        frozen_passes(0)
        adapter_pass(0)
        quantize_h(1)
        frozen_passes(1)
        adapter_pass(1)
        gate_y(0, 0, 4)
        gate_y(1, 3, 4)
        round_wa(1, 0, 84, "wa_raw01")
        quantize_wa(1, 0)
        h_pass(2, 0)
        h_pass(3, 0)
        round_wa(1, 1, P, "h_c0")
        quantize_wa(1, 1)
        h_pass(2, 1)
        h_pass(3, 1)
        gelu(2)
        gelu(3)
        deal_w_scales(1, "h_c0")
        quantize_h(2)
        frozen_passes(2)
        adapter_pass(2)
        gate_y(1, 0, 3, "wa_c11")
        quantize_h(3)
        frozen_passes(3)
        adapter_pass(3)
        gate_y(2, 0, 4)
        gate_y(3, 0, 4)
        for t in range(4):
            scatter(0, t, False)
        for t in (3, 0, 1, 2):
            scatter(1, t, False)
        for t in range(2):
            for b in range(2, 4):
                scatter(b, t, True)
                scatter(b, t + 2, False)

        out_rows = out_0.rearrange("(p t) c -> p t c", t=PACK)
        out_planes = tile("out_planes", [P, PACK, T], BF16)
        out_bf = tile("out_bf", [P, T, PACK], BF16)
        out_c = tile("out_c", [P, T], U32)
        out_s = tile("out_s", [P, T], U8)
        for t in (0, 2, 1, 3):
            nc.sync.dma_start(out_rows[:, t, :], out_sb[t][:])
        for t in (0, 2, 1, 3):
            nc.vector.tensor_copy(out_planes[:, t, :], out_sb[t][:])
        src = out_planes[:].rearrange("p t (c i) -> p c t i", i=PACK)
        dst = out_bf[:].rearrange("p (c i) t -> p c t i", i=PACK)
        nc.vector.tensor_copy(dst[:, :64], src[:, :64])
        nc.scalar.copy(dst[:, 96:], src[:, 96:])
        nc.vector.tensor_copy(dst[:, 64:96], src[:, 64:96])
        half = T // 2
        words = out_1[0].rearrange("p t d -> p (t d)").bitcast(I32)
        for i in range(2):
            cols = slice(i * half, (i + 1) * half)
            nc.vector.quantize_mx(
                out=out_c[:, cols].bitcast(FP8X4),
                scales=out_s[:, cols],
                in_=out_bf[:, cols, :].rearrange("p c t -> p (c t)"),
            )
            nc.sync.dma_start(words[:, cols], out_c[:, cols].bitcast(I32))
        for q in range(4):
            nc.scalar.dma_start(out_2[0, 4 * q : 4 * q + 4, :].bitcast(I32), out_s[32 * q : 32 * q + 4, :].bitcast(I32))
